import numpy as np
import ml_dtypes


def mxq(x, axis, fmt="e4m3"):
    dtype, down = {"e4m3": (ml_dtypes.float8_e4m3fn, 7), "e5m2": (ml_dtypes.float8_e5m2, 14)}[fmt]
    v = np.moveaxis(np.asarray(x, np.float32).astype(ml_dtypes.bfloat16).astype(np.float64), axis, -1)
    blocks = v.reshape(v.shape[:-1] + (-1, 32))
    amax = np.abs(blocks).max(-1, keepdims=True)
    byte = np.maximum(np.where(amax > 0, np.frexp(amax)[1] - 1 + 127, 0) - down, 1)
    scale = np.exp2(byte - 127.0)
    codes = (blocks / scale).astype(np.float32).astype(dtype).astype(np.float64)
    return np.moveaxis((codes * scale).reshape(v.shape), -1, axis)


WIDE = False


def mx_kscale(k):
    if not WIDE:
        return np.ones(k)
    levels = np.array([10, -10, 5, -5, 0])
    if k % 512:
        return np.exp2(np.random.permutation(np.resize(levels, k // 32))).repeat(32)
    a = np.empty((k // 512, 16))
    for p in range(k // 512):
        a[p, :8] = np.random.permutation(np.resize(levels, 8))
        for g in range(8):
            far = levels[np.abs(levels - a[p, g]) >= 10]
            a[p, g + 8] = far[np.random.randint(len(far))]
    return np.exp2(a.ravel()).repeat(32)


def f64(x):
    return np.asarray(x).astype(np.float64)


def striped(idx):
    return np.tile(idx.reshape(-1, 16).T, (8, 1)).astype(np.uint16)


def unstriped(offs):
    return offs[:16].T.reshape(-1).astype(np.int64)


E2M1 = np.array([0.0, 0.5, 1.0, 1.5, 2.0, 3.0, 4.0, 6.0, -0.0, -0.5, -1.0, -1.5, -2.0, -3.0, -4.0, -6.0])


def pack_weight(w, fmt):
    k, n = w.shape
    w = f64(np.asarray(w, np.float32).astype(ml_dtypes.bfloat16)).reshape(k // 32, 32, n)
    amax = np.abs(w).max(1)
    if fmt == "e4m3":
        byte = np.frexp(amax)[1] - 1 + 127 - 7
    else:
        mant, ex = np.frexp(amax / 6.0)
        byte = np.where(mant > 0.5, ex, ex - 1) + 127
    byte = np.clip(np.where(amax > 0, byte, 1), 1, 254)
    scaled = (w * np.exp2(127.0 - byte)[:, None, :]).reshape(k, n).astype(np.float32)
    by_word = np.ascontiguousarray(scaled.reshape(k // 512, 128, 4, n).transpose(0, 1, 3, 2))
    if fmt == "e4m3":
        words = by_word.astype(ml_dtypes.float8_e4m3fn).view(np.uint8)
    else:
        c = by_word.astype(ml_dtypes.float4_e2m1fn).view(np.uint8) & 0xF
        words = (c[..., 0::2] | (c[..., 1::2] << 4)).reshape(k // 512, 128, 2 * n)
    return np.ascontiguousarray(words), np.ascontiguousarray(byte.astype(np.uint8).reshape(k // 512, 16, n))


def unpack_weight(words, scales, fmt):
    g, _, n = scales.shape
    words = np.ascontiguousarray(words).reshape(g, 128, n, -1)
    if fmt == "e4m3":
        vals = words.view(ml_dtypes.float8_e4m3fn).astype(np.float64)
    else:
        nib = np.empty((g, 128, n, 4), np.uint8)
        nib[..., 0::2] = words & 0xF
        nib[..., 1::2] = words >> 4
        vals = E2M1[nib]
    vals = vals * np.repeat(np.exp2(scales.astype(np.float64) - 127.0), 8, axis=1)[..., None]
    return vals.transpose(0, 1, 3, 2).reshape(g * 512, n)


def relu(v):
    return np.maximum(v, 0.0)


K, T, E, C, N = 512, 1536, 12, 256, 128


def by_expert(wq, xq):
    return np.concatenate([wq[e].T @ xq[:, e * C:(e + 1) * C] for e in range(E)], axis=1)


def setup_inputs():
    n = np.random.standard_normal
    s = mx_kscale(K)[:, None]
    first = np.random.permutation(np.repeat(np.arange(E), T // E))
    second = (first + 1 + np.random.permutation(np.repeat(np.arange(E - 1), -(-T // (E - 1)))[:T])) % E
    while np.bincount(second, minlength=E).max() != T // E:
        load = np.bincount(second, minlength=E); hi, lo = int(load.argmax()), int(load.argmin())
        t = np.flatnonzero((second == hi) & (first != lo))[0]; second[t] = lo
    slot_token = np.empty(E * C, np.int64); pos = np.empty((2, T), np.int64); fill = np.zeros(E, np.int64)
    place = np.stack([np.random.permutation(C) for _ in range(E)])
    for r, deal in enumerate((first, second)):
        for t in np.random.permutation(T):
            e = deal[t]; j = e * C + place[e, fill[e]]; fill[e] += 1; slot_token[j] = t; pos[r, t] = j
    g = np.random.uniform(0.2, 0.8, T)
    w = [pack_weight(m, "e2m1") for m in n((E, K, N)) / np.sqrt(K) / s[None]]
    return {
        "xT": (n((K, T)) * s).astype(np.float32),
        "w_words": np.stack([m[0] for m in w]),
        "w_scales": np.stack([m[1] for m in w]),
        "b": (0.3 * n((N, E))).astype(np.float32),
        "gate": np.stack([np.tile(g, (N, 1)), np.tile(1.0 - g, (N, 1))]).astype(np.float32),
        "offs": striped(slot_token),
        "pos1": striped(pos[0]),
        "pos2": striped(pos[1]),
    }


def reference(xT, w_words, w_scales, b, gate, offs, pos1, pos2):
    idx = unstriped(offs)
    w = np.stack([unpack_weight(w_words[e], w_scales[e], "e2m1") for e in range(E)])
    xq = mxq(f64(xT)[:, idx], 0, "e4m3")
    y = by_expert(w, xq)
    y = relu(y + np.repeat(f64(b), C, axis=1))
    return f64(gate[0]) * y[:, unstriped(pos1)] + f64(gate[1]) * y[:, unstriped(pos2)]

@@ -1,0 +1,135 @@
+from contextlib import ExitStack
+
+import concourse.mybir as mybir
+
+K, T, E, C, N = 512, 1536, 12, 256, 128
+S = E * C
+P = 128
+PACK = 4
+FLOPS = 2 * K * N * S
+
+F32 = mybir.dt.float32
+BF16 = mybir.dt.bfloat16
+I32 = mybir.dt.int32
+U32 = mybir.dt.uint32
+U16 = mybir.dt.uint16
+U8 = mybir.dt.uint8
+FP8X4 = mybir.dt.float8_e4m3fn_x4
+FP4X4 = mybir.dt.float4_e2m1fn_x4
+COPY = mybir.ActivationFunctionType.Copy
+RELU = mybir.ActivationFunctionType.Relu
+ADD = mybir.AluOpType.add
+MULT = mybir.AluOpType.mult
+
+CHUNKS = (512, 512, 256, 128, 128)
+SCALAR_EIGHTHS = 3
+SLOT_RUNS = (1024, 1024, 768, 256)
+TOKEN_RUNS = (640, 512, 256, 128)
+
+
+def tile_moe_pln_lin_relu_kernel(tc, xT, w_words, w_scales, b, gate, offs, pos1, pos2, out):
+    nc = tc.nc
+    with ExitStack() as ctx:
+        keep = ctx.enter_context(tc.tile_pool(name="keep", bufs=1))
+        psum = ctx.enter_context(tc.psum_pool(name="psum", bufs=8))
+
+        raws = []
+        t0 = 0
+        for i, width in enumerate(CHUNKS):
+            raw = keep.tile([P, PACK, width], F32, name=f"raw{i}")
+            nc.sync.dma_start(out=raw[:], in_=xT[:, t0 : t0 + width].rearrange("(p j) t -> p j t", j=PACK))
+            raws.append(raw)
+            t0 += width
+
+        offs_sb = keep.tile([P, S // 16], U16, name="offs_sb")
+        nc.sync.dma_start(offs_sb[:], offs)
+
+        codes = keep.tile([P, T], U32, name="codes", align_bytes=64)
+        bytes_sb = keep.tile([P, T], U8, name="bytes_sb", align_bytes=64)
+        nc.gpsimd.memset(bytes_sb[:], 0)
+
+        w_plane = keep.tile([P, E, N], U8, name="w_plane", align_bytes=64)
+        nc.vector.memset(w_plane[:].rearrange("p e n -> p (e n)").bitcast(I32), 0)
+        for q in range(4):
+            nc.sync.dma_start(
+                out=w_plane[32 * q : 32 * q + 4].rearrange("p e n -> p (e n)").bitcast(I32).rearrange("p (e n) -> p e n", e=E),
+                in_=w_scales[:, 0, 4 * q : 4 * q + 4, :].bitcast(I32).rearrange("e r n -> r e n"),
+            )
+        w_codes = keep.tile([P, E, 2 * N], U8, name="w_codes", align_bytes=64)
+        nc.sync.dma_start(
+            out=w_codes[:].rearrange("p e x -> p (e x)").bitcast(I32).rearrange("p (e x) -> p e x", e=E),
+            in_=w_words[:, 0].bitcast(I32).rearrange("e p x -> p e x"),
+        )
+        bias = keep.tile([P, E], F32, name="bias")
+        nc.sync.dma_start(bias[:], b)
+        pos1_sb = keep.tile([P, T // 16], U16, name="pos1_sb")
+        nc.sync.dma_start(pos1_sb[:], pos1)
+        pos2_sb = keep.tile([P, T // 16], U16, name="pos2_sb")
+        nc.sync.dma_start(pos2_sb[:], pos2)
+        gates = keep.tile([P, 2, T], F32, name="gates")
+        nc.sync.dma_start(gates[:], gate.rearrange("r n t -> n r t"))
+
+        t0 = 0
+        for i, width in enumerate(CHUNKS):
+            grouped = keep.tile([P, width, PACK], BF16, name=f"grouped{i}", align_bytes=64)
+            cut = width - width * SCALAR_EIGHTHS // 8
+            for lo, hi in ((cut, width), (0, cut)):
+                src = raws[i][:, :, lo:hi].rearrange("p t (c i) -> p c t i", i=4)
+                dst = grouped[:, lo:hi, :].rearrange("p (c i) t -> p c t i", i=4)
+                if lo:
+                    nc.scalar.activation(dst, src, COPY)
+                else:
+                    nc.vector.tensor_copy(dst, src)
+            nc.vector.quantize_mx(
+                out=codes[:, t0 : t0 + width].bitcast(FP8X4),
+                scales=bytes_sb[:, t0 : t0 + width],
+                in_=grouped[:].rearrange("p t j -> p (t j)"),
+            )
+            t0 += width
+
+        y = keep.tile([P, S], F32, name="y")
+        s0 = 0
+        for i, count in enumerate(SLOT_RUNS):
+            slots = offs_sb[:, s0 // 16 : (s0 + count) // 16]
+            slot_codes = keep.tile([P, count], U32, name=f"slot_codes{i}", align_bytes=64)
+            nc.vector.tensor_copy(slot_codes[:], codes[:].indirect(slots))
+            slot_bytes = keep.tile([P, count], U8, name=f"slot_bytes{i}", align_bytes=64)
+            nc.vector.tensor_copy(slot_bytes[:], bytes_sb[:].indirect(slots))
+            for c0 in range(0, count, C):
+                e = (s0 + c0) // C
+                acc = psum.tile([N, C], F32, name="acc")
+                nc.tensor.matmul_mx(
+                    out=acc[:],
+                    lhsT=w_codes[:, e, :].bitcast(FP4X4),
+                    lhsT_scale=w_plane[:, e, :],
+                    rhs=slot_codes[:, c0 : c0 + C].bitcast(FP8X4),
+                    rhs_scale=slot_bytes[:, c0 : c0 + C],
+                    start=True,
+                    stop=True,
+                )
+                nc.scalar.activation(y[:, s0 + c0 : s0 + c0 + C], acc[:], RELU, bias=bias[:, e : e + 1])
+            s0 += count
+
+        def add_and_store(i, start, count, first, second):
+            total = keep.tile([P, count], F32, name=f"total{i}")
+            nc.vector.tensor_tensor(total[:], first[:], second[:], ADD)
+            nc.sync.dma_start(out=out[:, start : start + count], in_=total[:])
+
+        waiting = None
+        start = 0
+        for i, count in enumerate(TOKEN_RUNS):
+            picks = []
+            for r, lists in enumerate((pos1_sb, pos2_sb)):
+                pick = keep.tile([P, count], F32, name=f"pick{i}_{r}")
+                nc.vector.tensor_tensor(
+                    pick[:],
+                    y[:].indirect(lists[:, start // 16 : (start + count) // 16]),
+                    gates[:, r, start : start + count],
+                    MULT,
+                )
+                picks.append(pick)
+            if waiting is not None:
+                add_and_store(*waiting)
+            waiting = (i, start, count, picks[0], picks[1])
+            start += count
+        add_and_store(*waiting)

@@ -20,10 +20,15 @@ COPY = mybir.ActivationFunctionType.Copy
 RELU = mybir.ActivationFunctionType.Relu
 ADD = mybir.AluOpType.add
 MULT = mybir.AluOpType.mult
+MAX = mybir.AluOpType.max
 
 CHUNKS = (512, 512, 256, 128, 128)
 SCALAR_EIGHTHS = 3
-SLOT_RUNS = (1024, 1024, 768, 256)
+GATHERS = (
+    ("codes", 0, 1152), ("bytes", 0, 1152),
+    ("codes", 1152, 2304), ("bytes", 1152, 2304),
+    ("codes", 2304, 3072), ("bytes", 2304, 2816), ("bytes", 2816, 3072),
+)
 TOKEN_RUNS = (640, 512, 256, 128)
 
 
@@ -69,8 +74,7 @@ def tile_moe_pln_lin_relu_kernel(tc, xT, w_words, w_scales, b, gate, offs, pos1,
         gates = keep.tile([P, 2, T], F32, name="gates")
         nc.sync.dma_start(gates[:], gate.rearrange("r n t -> n r t"))
 
-        t0 = 0
-        for i, width in enumerate(CHUNKS):
+        def interleave(i, width):
             grouped = keep.tile([P, width, PACK], BF16, name=f"grouped{i}", align_bytes=64)
             cut = width - width * SCALAR_EIGHTHS // 8
             for lo, hi in ((cut, width), (0, cut)):
@@ -80,56 +84,84 @@ def tile_moe_pln_lin_relu_kernel(tc, xT, w_words, w_scales, b, gate, offs, pos1,
                     nc.scalar.activation(dst, src, COPY)
                 else:
                     nc.vector.tensor_copy(dst, src)
+            return grouped
+
+        def quantise(grouped, start, width):
             nc.vector.quantize_mx(
-                out=codes[:, t0 : t0 + width].bitcast(FP8X4),
-                scales=bytes_sb[:, t0 : t0 + width],
+                out=codes[:, start : start + width].bitcast(FP8X4),
+                scales=bytes_sb[:, start : start + width],
                 in_=grouped[:].rearrange("p t j -> p (t j)"),
             )
-            t0 += width
 
+        start = 0
+        held = None
+        for i, width in enumerate(CHUNKS):
+            grouped = interleave(i, width)
+            if held is not None:
+                quantise(*held)
+            held = (grouped, start, width)
+            start += width
+        quantise(*held)
+
+        slot_codes = keep.tile([P, S], U32, name="slot_codes", align_bytes=64)
+        slot_bytes = keep.tile([P, S], U8, name="slot_bytes", align_bytes=64)
         y = keep.tile([P, S], F32, name="y")
-        s0 = 0
-        for i, count in enumerate(SLOT_RUNS):
-            slots = offs_sb[:, s0 // 16 : (s0 + count) // 16]
-            slot_codes = keep.tile([P, count], U32, name=f"slot_codes{i}", align_bytes=64)
-            nc.vector.tensor_copy(slot_codes[:], codes[:].indirect(slots))
-            slot_bytes = keep.tile([P, count], U8, name=f"slot_bytes{i}", align_bytes=64)
-            nc.vector.tensor_copy(slot_bytes[:], bytes_sb[:].indirect(slots))
-            for c0 in range(0, count, C):
-                e = (s0 + c0) // C
-                acc = psum.tile([N, C], F32, name="acc")
-                nc.tensor.matmul_mx(
-                    out=acc[:],
-                    lhsT=w_codes[:, e, :].bitcast(FP4X4),
-                    lhsT_scale=w_plane[:, e, :],
-                    rhs=slot_codes[:, c0 : c0 + C].bitcast(FP8X4),
-                    rhs_scale=slot_bytes[:, c0 : c0 + C],
-                    start=True,
-                    stop=True,
-                )
-                nc.scalar.activation(y[:, s0 + c0 : s0 + c0 + C], acc[:], RELU, bias=bias[:, e : e + 1])
-            s0 += count
 
-        def add_and_store(i, start, count, first, second):
-            total = keep.tile([P, count], F32, name=f"total{i}")
-            nc.vector.tensor_tensor(total[:], first[:], second[:], ADD)
+        def multiply(e, s0, count):
+            acc = psum.tile([N, count], F32, name="acc")
+            nc.tensor.matmul_mx(
+                out=acc[:],
+                lhsT=w_codes[:, e, :].bitcast(FP4X4),
+                lhsT_scale=w_plane[:, e, :],
+                rhs=slot_codes[:, s0 : s0 + count].bitcast(FP8X4),
+                rhs_scale=slot_bytes[:, s0 : s0 + count],
+                start=True,
+                stop=True,
+            )
+            return acc
+
+        multiplied = 0
+        for kind, lo, hi in GATHERS:
+            held, table = (slot_codes, codes) if kind == "codes" else (slot_bytes, bytes_sb)
+            nc.vector.tensor_copy(held[:, lo:hi], table[:].indirect(offs_sb[:, lo // 16 : hi // 16]))
+            if kind == "codes":
+                continue
+            while multiplied < E - 1 and (multiplied + 1) * C <= hi:
+                s0 = multiplied * C
+                acc = multiply(multiplied, s0, C)
+                nc.scalar.activation(y[:, s0 : s0 + C], acc[:], RELU, bias=bias[:, multiplied : multiplied + 1])
+                multiplied += 1
+        half = C // 2
+        s0 = S - C
+        acc = multiply(E - 1, s0, half)
+        nc.scalar.activation(y[:, s0 : s0 + half], acc[:], RELU, bias=bias[:, E - 1 : E])
+        s0 += half
+        acc = multiply(E - 1, s0, half)
+        nc.vector.tensor_scalar(y[:, s0 : s0 + half], acc[:], bias[:, E - 1 : E], 0.0, ADD, MAX)
+
+        def pick(r, start, count):
+            picked = keep.tile([P, count], F32, name=f"picked{r}_{start}")
+            lists = (pos1_sb, pos2_sb)[r]
+            nc.vector.tensor_tensor(
+                picked[:],
+                y[:].indirect(lists[:, start // 16 : (start + count) // 16]),
+                gates[:, r, start : start + count],
+                MULT,
+            )
+            return picked
+
+        def add_and_store(start, count, second):
+            total = keep.tile([P, count], F32, name=f"total{start}")
+            nc.vector.tensor_tensor(total[:], first[:, start : start + count], second[:], ADD)
             nc.sync.dma_start(out=out[:, start : start + count], in_=total[:])
 
+        first = pick(0, 0, T)
         waiting = None
         start = 0
-        for i, count in enumerate(TOKEN_RUNS):
-            picks = []
-            for r, lists in enumerate((pos1_sb, pos2_sb)):
-                pick = keep.tile([P, count], F32, name=f"pick{i}_{r}")
-                nc.vector.tensor_tensor(
-                    pick[:],
-                    y[:].indirect(lists[:, start // 16 : (start + count) // 16]),
-                    gates[:, r, start : start + count],
-                    MULT,
-                )
-                picks.append(pick)
+        for count in TOKEN_RUNS:
+            second = pick(1, start, count)
             if waiting is not None:
                 add_and_store(*waiting)
-            waiting = (i, start, count, picks[0], picks[1])
+            waiting = (start, count, second)
             start += count
         add_and_store(*waiting)

@@ -20,9 +20,8 @@ COPY = mybir.ActivationFunctionType.Copy
 RELU = mybir.ActivationFunctionType.Relu
 ADD = mybir.AluOpType.add
 MULT = mybir.AluOpType.mult
-MAX = mybir.AluOpType.max
 
-CHUNKS = (512, 512, 256, 128, 128)
+CHUNKS = (256, 256, 256, 256, 256, 128, 128)
 SCALAR_EIGHTHS = 3
 GATHERS = (
     ("codes", 0, 1152), ("bytes", 0, 1152),
@@ -94,14 +93,9 @@ def tile_moe_pln_lin_relu_kernel(tc, xT, w_words, w_scales, b, gate, offs, pos1,
             )
 
         start = 0
-        held = None
         for i, width in enumerate(CHUNKS):
-            grouped = interleave(i, width)
-            if held is not None:
-                quantise(*held)
-            held = (grouped, start, width)
+            quantise(interleave(i, width), start, width)
             start += width
-        quantise(*held)
 
         slot_codes = keep.tile([P, S], U32, name="slot_codes", align_bytes=64)
         slot_bytes = keep.tile([P, S], U8, name="slot_bytes", align_bytes=64)
@@ -137,7 +131,7 @@ def tile_moe_pln_lin_relu_kernel(tc, xT, w_words, w_scales, b, gate, offs, pos1,
         nc.scalar.activation(y[:, s0 : s0 + half], acc[:], RELU, bias=bias[:, E - 1 : E])
         s0 += half
         acc = multiply(E - 1, s0, half)
-        nc.vector.tensor_scalar(y[:, s0 : s0 + half], acc[:], bias[:, E - 1 : E], 0.0, ADD, MAX)
+        nc.scalar.activation(y[:, s0 : s0 + half], acc[:], RELU, bias=bias[:, E - 1 : E])
 
         def pick(r, start, count):
             picked = keep.tile([P, count], F32, name=f"picked{r}_{start}")

@@ -21,8 +21,8 @@ RELU = mybir.ActivationFunctionType.Relu
 ADD = mybir.AluOpType.add
 MULT = mybir.AluOpType.mult
 
-CHUNKS = (256, 256, 256, 256, 256, 128, 128)
-SCALAR_EIGHTHS = 3
+CHUNKS = (512, 512, 256, 256)
+SCALAR_EIGHTHS = (4, 4, 4, 3)
 GATHERS = (
     ("codes", 0, 1152), ("bytes", 0, 1152),
     ("codes", 1152, 2304), ("bytes", 1152, 2304),
@@ -75,7 +75,7 @@ def tile_moe_pln_lin_relu_kernel(tc, xT, w_words, w_scales, b, gate, offs, pos1,
 
         def interleave(i, width):
             grouped = keep.tile([P, width, PACK], BF16, name=f"grouped{i}", align_bytes=64)
-            cut = width - width * SCALAR_EIGHTHS // 8
+            cut = width - width * SCALAR_EIGHTHS[i] // 8
             for lo, hi in ((cut, width), (0, cut)):
                 src = raws[i][:, :, lo:hi].rearrange("p t (c i) -> p c t i", i=4)
                 dst = grouped[:, lo:hi, :].rearrange("p (c i) t -> p c t i", i=4)

from contextlib import ExitStack

import concourse.mybir as mybir

K, T, E, C, N = 512, 1536, 12, 256, 128
S = E * C
P = 128
PACK = 4
FLOPS = 2 * K * N * S

F32 = mybir.dt.float32
BF16 = mybir.dt.bfloat16
I32 = mybir.dt.int32
U32 = mybir.dt.uint32
U16 = mybir.dt.uint16
U8 = mybir.dt.uint8
FP8X4 = mybir.dt.float8_e4m3fn_x4
FP4X4 = mybir.dt.float4_e2m1fn_x4
COPY = mybir.ActivationFunctionType.Copy
RELU = mybir.ActivationFunctionType.Relu
ADD = mybir.AluOpType.add
MULT = mybir.AluOpType.mult

CHUNKS = (512, 512, 256, 256)
SCALAR_EIGHTHS = (4, 4, 4, 3)
GATHERS = (
    ("codes", 0, 1152), ("bytes", 0, 1152),
    ("codes", 1152, 2304), ("bytes", 1152, 2304),
    ("codes", 2304, 3072), ("bytes", 2304, 2816), ("bytes", 2816, 3072),
)
TOKEN_RUNS = (640, 512, 256, 128)


def tile_moe_pln_lin_relu_kernel(tc, xT, w_words, w_scales, b, gate, offs, pos1, pos2, out):
    nc = tc.nc
    with ExitStack() as ctx:
        keep = ctx.enter_context(tc.tile_pool(name="keep", bufs=1))
        psum = ctx.enter_context(tc.psum_pool(name="psum", bufs=8))

        raws = []
        t0 = 0
        for i, width in enumerate(CHUNKS):
            raw = keep.tile([P, PACK, width], F32, name=f"raw{i}")
            nc.sync.dma_start(out=raw[:], in_=xT[:, t0 : t0 + width].rearrange("(p j) t -> p j t", j=PACK))
            raws.append(raw)
            t0 += width

        offs_sb = keep.tile([P, S // 16], U16, name="offs_sb")
        nc.sync.dma_start(offs_sb[:], offs)

        codes = keep.tile([P, T], U32, name="codes", align_bytes=64)
        bytes_sb = keep.tile([P, T], U8, name="bytes_sb", align_bytes=64)
        nc.gpsimd.memset(bytes_sb[:], 0)

        w_plane = keep.tile([P, E, N], U8, name="w_plane", align_bytes=64)
        nc.vector.memset(w_plane[:].rearrange("p e n -> p (e n)").bitcast(I32), 0)
        for q in range(4):
            nc.sync.dma_start(
                out=w_plane[32 * q : 32 * q + 4].rearrange("p e n -> p (e n)").bitcast(I32).rearrange("p (e n) -> p e n", e=E),
                in_=w_scales[:, 0, 4 * q : 4 * q + 4, :].bitcast(I32).rearrange("e r n -> r e n"),
            )
        w_codes = keep.tile([P, E, 2 * N], U8, name="w_codes", align_bytes=64)
        nc.sync.dma_start(
            out=w_codes[:].rearrange("p e x -> p (e x)").bitcast(I32).rearrange("p (e x) -> p e x", e=E),
            in_=w_words[:, 0].bitcast(I32).rearrange("e p x -> p e x"),
        )
        bias = keep.tile([P, E], F32, name="bias")
        nc.sync.dma_start(bias[:], b)
        pos1_sb = keep.tile([P, T // 16], U16, name="pos1_sb")
        nc.sync.dma_start(pos1_sb[:], pos1)
        pos2_sb = keep.tile([P, T // 16], U16, name="pos2_sb")
        nc.sync.dma_start(pos2_sb[:], pos2)
        gates = keep.tile([P, 2, T], F32, name="gates")
        nc.sync.dma_start(gates[:], gate.rearrange("r n t -> n r t"))

        def interleave(i, width):
            grouped = keep.tile([P, width, PACK], BF16, name=f"grouped{i}", align_bytes=64)
            cut = width - width * SCALAR_EIGHTHS[i] // 8
            for lo, hi in ((cut, width), (0, cut)):
                src = raws[i][:, :, lo:hi].rearrange("p t (c i) -> p c t i", i=4)
                dst = grouped[:, lo:hi, :].rearrange("p (c i) t -> p c t i", i=4)
                if lo:
                    nc.scalar.activation(dst, src, COPY)
                else:
                    nc.vector.tensor_copy(dst, src)
            return grouped

        def quantise(grouped, start, width):
            nc.vector.quantize_mx(
                out=codes[:, start : start + width].bitcast(FP8X4),
                scales=bytes_sb[:, start : start + width],
                in_=grouped[:].rearrange("p t j -> p (t j)"),
            )

        start = 0
        for i, width in enumerate(CHUNKS):
            quantise(interleave(i, width), start, width)
            start += width

        slot_codes = keep.tile([P, S], U32, name="slot_codes", align_bytes=64)
        slot_bytes = keep.tile([P, S], U8, name="slot_bytes", align_bytes=64)
        y = keep.tile([P, S], F32, name="y")

        def multiply(e, s0, count):
            acc = psum.tile([N, count], F32, name="acc")
            nc.tensor.matmul_mx(
                out=acc[:],
                lhsT=w_codes[:, e, :].bitcast(FP4X4),
                lhsT_scale=w_plane[:, e, :],
                rhs=slot_codes[:, s0 : s0 + count].bitcast(FP8X4),
                rhs_scale=slot_bytes[:, s0 : s0 + count],
                start=True,
                stop=True,
            )
            return acc

        multiplied = 0
        for kind, lo, hi in GATHERS:
            held, table = (slot_codes, codes) if kind == "codes" else (slot_bytes, bytes_sb)
            nc.vector.tensor_copy(held[:, lo:hi], table[:].indirect(offs_sb[:, lo // 16 : hi // 16]))
            if kind == "codes":
                continue
            while multiplied < E - 1 and (multiplied + 1) * C <= hi:
                s0 = multiplied * C
                acc = multiply(multiplied, s0, C)
                nc.scalar.activation(y[:, s0 : s0 + C], acc[:], RELU, bias=bias[:, multiplied : multiplied + 1])
                multiplied += 1
        half = C // 2
        s0 = S - C
        acc = multiply(E - 1, s0, half)
        nc.scalar.activation(y[:, s0 : s0 + half], acc[:], RELU, bias=bias[:, E - 1 : E])
        s0 += half
        acc = multiply(E - 1, s0, half)
        nc.scalar.activation(y[:, s0 : s0 + half], acc[:], RELU, bias=bias[:, E - 1 : E])

        def pick(r, start, count):
            picked = keep.tile([P, count], F32, name=f"picked{r}_{start}")
            lists = (pos1_sb, pos2_sb)[r]
            nc.vector.tensor_tensor(
                picked[:],
                y[:].indirect(lists[:, start // 16 : (start + count) // 16]),
                gates[:, r, start : start + count],
                MULT,
            )
            return picked

        def add_and_store(start, count, second):
            total = keep.tile([P, count], F32, name=f"total{start}")
            nc.vector.tensor_tensor(total[:], first[:, start : start + count], second[:], ADD)
            nc.sync.dma_start(out=out[:, start : start + count], in_=total[:])

        first = pick(0, 0, T)
        waiting = None
        start = 0
        for count in TOKEN_RUNS:
            second = pick(1, start, count)
            if waiting is not None:
                add_and_store(*waiting)
            waiting = (start, count, second)
            start += count
        add_and_store(*waiting)
